import numpy as np
import ml_dtypes


def mxq(x, axis, fmt="e4m3"):
    dtype, down = {"e4m3": (ml_dtypes.float8_e4m3fn, 7), "e5m2": (ml_dtypes.float8_e5m2, 14)}[fmt]
    v = np.moveaxis(np.asarray(x, np.float32).astype(ml_dtypes.bfloat16).astype(np.float64), axis, -1)
    blocks = v.reshape(v.shape[:-1] + (-1, 32))
    amax = np.abs(blocks).max(-1, keepdims=True)
    byte = np.maximum(np.where(amax > 0, np.frexp(amax)[1] - 1 + 127, 0) - down, 1)
    scale = np.exp2(byte - 127.0)
    codes = (blocks / scale).astype(np.float32).astype(dtype).astype(np.float64)
    return np.moveaxis((codes * scale).reshape(v.shape), -1, axis)


WIDE = False


def mx_kscale(k):
    if not WIDE:
        return np.ones(k)
    levels = np.array([10, -10, 5, -5, 0])
    if k % 512:
        return np.exp2(np.random.permutation(np.resize(levels, k // 32))).repeat(32)
    a = np.empty((k // 512, 16))
    for p in range(k // 512):
        a[p, :8] = np.random.permutation(np.resize(levels, 8))
        for g in range(8):
            far = levels[np.abs(levels - a[p, g]) >= 10]
            a[p, g + 8] = far[np.random.randint(len(far))]
    return np.exp2(a.ravel()).repeat(32)


def f64(x):
    return np.asarray(x).astype(np.float64)


def striped(idx):
    return np.tile(idx.reshape(-1, 16).T, (8, 1)).astype(np.uint16)


def unstriped(offs):
    return offs[:16].T.reshape(-1).astype(np.int64)


def striped8(idx):
    return np.concatenate([x.reshape(-1, 16).T for x in idx]).astype(np.uint16)


def runs(offs, k):
    lists = np.stack([offs[16 * r : 16 * r + 16].T.reshape(-1) for r in range(8)]).astype(np.int64)
    return lists[np.arange(k) % 512 // 64]


def pack_weight(w):
    k, n = w.shape
    w = f64(np.asarray(w, np.float32).astype(ml_dtypes.bfloat16)).reshape(k // 32, 32, n)
    amax = np.abs(w).max(1)
    byte = np.clip(np.where(amax > 0, np.frexp(amax)[1] - 1 + 127 - 7, 1), 1, 254)
    scaled = (w * np.exp2(127.0 - byte)[:, None, :]).reshape(k, n).astype(np.float32)
    words = np.ascontiguousarray(scaled.reshape(k // 512, 128, 4, n).transpose(0, 1, 3, 2)).astype(ml_dtypes.float8_e4m3fn).view(np.uint8)
    return words, np.ascontiguousarray(byte.astype(np.uint8).reshape(k // 512, 16, n))


def unpack_weight(words, scales):
    g, p, n, _ = words.shape
    vals = np.ascontiguousarray(words).view(ml_dtypes.float8_e4m3fn).astype(np.float64) * np.repeat(np.exp2(scales.astype(np.float64) - 127.0), 8, axis=1)[..., None]
    return vals.transpose(0, 1, 3, 2).reshape(g * 512, n)


def relu(v):
    return np.maximum(v, 0.0)


K, T, S, N, H, G = 512, 2048, 512, 512, 512, 2048


def setup_inputs():
    n = np.random.standard_normal
    s = mx_kscale(K)[:, None]
    u = mx_kscale(S)
    packed_xT = pack_weight(n((K, T)) * s)
    packed_dT = pack_weight(n((K, G)) / s)
    return {
        "x_words": packed_xT[0],
        "x_scales": packed_xT[1],
        "w1": (n((K, H)) / np.sqrt(K) / s).astype(np.float32),
        "d_words": packed_dT[0],
        "d_scales": packed_dT[1],
        "gn": (np.random.uniform(0.5, 1.5, (H, 1)) * u[:, None]).astype(np.float32),
        "w2": (n((H, N)) / np.sqrt(H) / u[:, None]).astype(np.float32),
        "offs": striped(np.random.permutation(T)[:S]),
        "k1": striped8(np.random.randint(0, G, (8, H))),
        "two": striped(np.random.permutation(T)[:S]),
        "n1": striped8(np.stack([np.random.permutation(S) for _ in range(8)])),
        "n2": striped8(np.stack([np.random.permutation(S) for _ in range(8)])),
        "n3": striped8(np.stack([np.random.permutation(S) for _ in range(8)])),
        "n4": striped8(np.stack([np.random.permutation(S) for _ in range(8)])),
        "n5": striped8(np.stack([np.random.permutation(S) for _ in range(8)])),
        "n6": striped8(np.stack([np.random.permutation(S) for _ in range(8)])),
    }


def reference(x_words, x_scales, w1, d_words, d_scales, gn, w2, offs, k1, two, n1, n2, n3, n4, n5, n6):
    xq = unpack_weight(x_words, x_scales)[:, unstriped(offs)]
    y = mxq(f64(w1), 0, "e4m3").T @ xq
    d_k1 = unpack_weight(d_words, d_scales)[np.arange(K)[:, None], runs(k1, K)]
    x_two = unpack_weight(x_words, x_scales)[:, unstriped(two)]
    d = 0.0625 * (d_k1.T @ x_two)
    z = f64(gn) * (np.maximum(y[np.arange(H)[:, None], runs(n1, H)] + d[np.arange(H)[:, None], runs(n3, H)], y[np.arange(H)[:, None], runs(n2, H)] + d[np.arange(H)[:, None], runs(n4, H)]))
    h = mxq(f64(w2), 0, "e4m3").T @ mxq(z, 0, "e4m3")
    return relu(h - (h[np.arange(N)[:, None], runs(n5, N)])) + 0.5 * (relu(h[np.arange(N)[:, None], runs(n6, N)] - h))

@@ -1,0 +1,206 @@
+from contextlib import ExitStack
+
+import concourse.mybir as mybir
+
+K, T, S, H, N = 512, 2048, 512, 512, 512
+FLOPS = 3 * 2 * 512 * 512 * 512
+
+F32 = mybir.dt.float32
+BF16 = mybir.dt.bfloat16
+I32 = mybir.dt.int32
+U32 = mybir.dt.uint32
+U16 = mybir.dt.uint16
+U8 = mybir.dt.uint8
+FP8X4 = mybir.dt.float8_e4m3fn_x4
+ALU = mybir.AluOpType
+ACT = mybir.ActivationFunctionType
+
+P = 128
+PACK = 4
+MID = (256, 128, 128)
+YG_BUFS = 4
+DG_BUFS = 3
+LAST = (256, 128, 128)
+WIDE = 256
+LIST_COL = 16
+
+
+def tile_picked_twkeypathbhinge_none_p_kernel(tc, x_words, x_scales, w1, d_words, d_scales, gn, w2, offs, k1, two, n1, n2, n3, n4, n5, n6, out):
+    nc = tc.nc
+    with ExitStack() as ctx:
+        keep = ctx.enter_context(tc.tile_pool(name="keep", bufs=1))
+        psum = ctx.enter_context(tc.psum_pool(name="psum", bufs=1))
+
+        def load_list(name, src):
+            tile = keep.tile([P, S // LIST_COL], U16, name=name)
+            nc.sync.dma_start(tile[:], src)
+            return tile
+
+        def load_words(name, src):
+            tile = keep.tile([P, T], U32, name=name, align_bytes=64)
+            nc.sync.dma_start(tile[:].bitcast(I32), src[0].rearrange("p c r -> p (c r)").bitcast(I32))
+            return tile
+
+        def load_weight(name, src):
+            tile = keep.tile([P, PACK, H], F32, name=name, align_bytes=64)
+            nc.sync.dma_start(tile[:], src.rearrange("(p j) c -> p j c", j=PACK))
+            return tile
+
+        k1_t = load_list("k1_t", k1)
+        d_bytes = keep.tile([P, T], U8, name="d_bytes", align_bytes=64)
+        nc.sync.dma_start(d_bytes[:].bitcast(I32), d_scales[0].bitcast(I32).unsqueeze(1).to_broadcast([16, 8, T // 4]))
+        offs_t = load_list("offs_t", offs)
+        x_bytes = keep.tile([P, T], U8, name="x_bytes", align_bytes=64)
+        for q in range(4):
+            nc.sync.dma_start(
+                x_bytes[32 * q : 32 * q + 32, :].bitcast(I32),
+                x_scales[0, 4 * q : 4 * q + 4, :].bitcast(I32).unsqueeze(0).to_broadcast([8, 4, T // 4]),
+            )
+        w1_raw = load_weight("w1_raw", w1)
+        x_table = load_words("x_table", x_words)
+        two_t = load_list("two_t", two)
+        d_table = load_words("d_table", d_words)
+        n3_t = load_list("n3_t", n3)
+        n1_t = load_list("n1_t", n1)
+        n4_t = load_list("n4_t", n4)
+        n2_t = load_list("n2_t", n2)
+        gain = keep.tile([P, PACK], F32, name="gain")
+        nc.sync.dma_start(gain[:], gn.rearrange("(p t) o -> p (t o)", t=PACK))
+        w2_raw = load_weight("w2_raw", w2)
+        n5_t = load_list("n5_t", n5)
+        n6_t = load_list("n6_t", n6)
+
+        def pick(name, table, offsets, dtype, tag=None):
+            tile = keep.tile([P, S], dtype, name=name, tag=tag or name, align_bytes=64)
+            nc.vector.tensor_copy(tile[:], table[:].indirect(offsets[:]))
+            return tile
+
+        def deal(name, picked, dtype):
+            tile = keep.tile([P, S], dtype, name=name, align_bytes=64)
+            nc.vector.tensor_copy(tile[:].rearrange("p (t m) -> p m t", t=PACK), picked[:].rearrange("p (m t) -> p m t", t=PACK))
+            return tile
+
+        def round_weight(copy, name, raw, tag):
+            tile = keep.tile([P, PACK * H], BF16, name=name, tag=tag, align_bytes=64)
+            copy(
+                tile[:].rearrange("p (t m j) -> p m j t", t=PACK, j=PACK),
+                raw[:].rearrange("p j (m t) -> p m j t", t=PACK),
+            )
+            return tile
+
+        def quantize(name, rounded, width):
+            codes = keep.tile([P, width], U32, name=name + "_codes", align_bytes=64)
+            scales = keep.tile([P, width], U8, name=name + "_scales", align_bytes=64)
+            nc.vector.quantize_mx(out=codes[:].bitcast(FP8X4), scales=scales[:], in_=rounded[:])
+            return codes, scales
+
+        def product(bank_cols, lhs, t, rhs):
+            cols = slice(P * t, P * (t + 1))
+            nc.tensor.matmul_mx(
+                out=bank_cols,
+                lhsT=lhs[0][:, cols].bitcast(FP8X4),
+                lhsT_scale=lhs[1][:, cols],
+                rhs=rhs[0][:].bitcast(FP8X4),
+                rhs_scale=rhs[1][:],
+                start=True,
+                stop=True,
+            )
+
+        def entries(offsets, lo, width):
+            return offsets[:, lo // LIST_COL : (lo + width) // LIST_COL]
+
+        dk_bytes_picked = pick("dk_bytes_picked", d_bytes, k1_t, U8)
+        dk_bytes = deal("dk_bytes", dk_bytes_picked, U8)
+        for e in range(1, 4):
+            nc.sync.dma_start(dk_bytes[e:P:32, :].bitcast(I32), dk_bytes[8 * e : P : 32, :].bitcast(I32))
+        xo_bytes = pick("xo_bytes", x_bytes, offs_t, U8)
+        w1_bf = round_weight(nc.scalar.copy, "w1_bf", w1_raw, "w1_bf")
+        xt_bytes = pick("xt_bytes", x_bytes, two_t, U8)
+        xo_words = pick("xo_words", x_table, offs_t, U32)
+        w1_q = quantize("w1", w1_bf, H)
+
+        y_sb, d_sb = [], []
+        for t in range(PACK):
+            bank = psum.tile([P, S], F32, name="ybank%d" % t, tag="bank%d" % t)
+            product(bank[:], w1_q, t, (xo_words, xo_bytes))
+            tile = keep.tile([P, S], F32, name="y%d" % t, align_bytes=64)
+            nc.scalar.copy(tile[:], bank[:])
+            y_sb.append(tile)
+
+        xt_words = pick("xt_words", x_table, two_t, U32, "w1_bf")
+        dk_words_picked = pick("dk_words_picked", d_table, k1_t, U32, "x_table")
+        dk_words = deal("dk_words", dk_words_picked, U32)
+        w2_bf = round_weight(nc.vector.tensor_copy, "w2_bf", w2_raw, "d_table")
+        w2_q = quantize("w2", w2_bf, N)
+        for t in range(PACK):
+            bank = psum.tile([P, S], F32, name="dbank%d" % t, tag="bank%d" % (PACK + t))
+            product(bank[:], (dk_words, dk_bytes), t, (xt_words, xt_bytes))
+            tile = keep.tile([P, S], F32, name="d%d" % t, align_bytes=64)
+            if t < 1:
+                nc.vector.tensor_scalar(tile[:], bank[:], 0.0625, None, ALU.mult)
+            else:
+                nc.scalar.activation(tile[:], bank[:], ACT.Copy, scale=0.0625)
+            d_sb.append(tile)
+
+        h_banks = [psum.tile([P, S], F32, name="hbank%d" % t, tag="bank%d" % t) for t in range(PACK)]
+        h_sb = [keep.tile([P, S], F32, name="h%d" % t, align_bytes=64) for t in range(PACK)]
+        lo = 0
+        for c, width in enumerate(MID):
+            cols = slice(lo, lo + width)
+            larger = keep.tile([P, PACK, width], F32, name="larger%d" % c, align_bytes=64)
+            for t in range(PACK):
+                sums = []
+                for u, (ny, nd) in enumerate(((n1_t, n3_t), (n2_t, n4_t))):
+                    yg = keep.tile([P, width], F32, name="yg", tag="yg", bufs=YG_BUFS, align_bytes=64)
+                    nc.scalar.activation(yg[:], y_sb[t][:].indirect(entries(ny, lo, width)), ACT.Copy)
+                    sm = keep.tile([P, width], F32, name="sum", tag="sum", bufs=4, align_bytes=64)
+                    if c == 0 or (u == 0 and t % 2 == 0):
+                        nc.vector.tensor_tensor(sm[:], d_sb[t][:].indirect(entries(nd, lo, width)), yg[:], ALU.add)
+                    else:
+                        dg = keep.tile([P, width], F32, name="dg", tag="dg", bufs=DG_BUFS, align_bytes=64)
+                        nc.scalar.activation(dg[:], d_sb[t][:].indirect(entries(nd, lo, width)), ACT.Copy)
+                        nc.vector.tensor_tensor(sm[:], dg[:], yg[:], ALU.add)
+                    sums.append(sm)
+                nc.vector.tensor_tensor(larger[:, t, :], sums[0][:], sums[1][:], ALU.max)
+            z_bf = keep.tile([P, PACK * width], BF16, name="z_bf%d" % c, align_bytes=64)
+            nc.vector.tensor_tensor(
+                z_bf[:].rearrange("p (b i t) -> p b t i", i=4, t=PACK),
+                larger[:].rearrange("p t (b i) -> p b t i", i=4),
+                gain[:].unsqueeze(1).unsqueeze(3).to_broadcast([P, width // 4, PACK, 4]),
+                ALU.mult,
+            )
+            z_q = quantize("z%d" % c, z_bf, width)
+            for t in range(PACK):
+                product(h_banks[t][:, cols], w2_q, t, z_q)
+                nc.scalar.activation(h_sb[t][:, cols], h_banks[t][:, cols], ACT.Copy, scale=-1.0)
+            lo = lo + width
+
+        out_rows = out.rearrange("(p t) j -> p t j", t=PACK)
+        pieces = []
+        for t in range(PACK):
+            lo = 0
+            for width in (LAST if t == PACK - 1 else (WIDE, WIDE)):
+                pieces.append((t, lo, width))
+                lo = lo + width
+
+        def finish(k, t, lo, width, diff, half):
+            res = keep.tile([P, width], F32, name="res%d" % k, align_bytes=64)
+            nc.vector.scalar_tensor_tensor(res[:], diff[:, 0, :], 0.0, half[:], ALU.max, ALU.add)
+            nc.sync.dma_start(out_rows[:, t, lo : lo + width], res[:])
+
+        pending = None
+        for k, (t, lo, width) in enumerate(pieces):
+            got = keep.tile([P, 2, width], F32, name="got%d" % k, align_bytes=64)
+            if k < 2 or k == len(pieces) - 1:
+                nc.vector.tensor_copy(got[:, 0, :], h_sb[t][:].indirect(entries(n5_t, lo, width)))
+            else:
+                nc.scalar.activation(got[:, 0, :], h_sb[t][:].indirect(entries(n5_t, lo, width)), ACT.Copy)
+            nc.scalar.activation(got[:, 1, :], h_sb[t][:].indirect(entries(n6_t, lo, width)), ACT.Copy)
+            diff = keep.tile([P, 2, width], F32, name="diff%d" % k, align_bytes=64)
+            nc.vector.tensor_tensor(diff[:], got[:], h_sb[t][:, lo : lo + width].unsqueeze(1).to_broadcast([P, 2, width]), ALU.subtract)
+            if pending is not None:
+                finish(*pending)
+            half = keep.tile([P, width], F32, name="half%d" % k, align_bytes=64)
+            nc.vector.tensor_scalar(half[:], diff[:, 1, :], 0.0, -0.5, ALU.min, ALU.mult)
+            pending = (k, t, lo, width, diff, half)
+        finish(*pending)

@@ -17,11 +17,11 @@ ACT = mybir.ActivationFunctionType
 
 P = 128
 PACK = 4
-MID = (256, 128, 128)
-YG_BUFS = 4
-DG_BUFS = 3
+MID = ((256,), (128, 128))
+WHOLE = 2
+HALF = 256
+GOT_BUFS = 4
 LAST = (256, 128, 128)
-WIDE = 256
 LIST_COL = 16
 
 
@@ -41,8 +41,8 @@ def tile_picked_twkeypathbhinge_none_p_kernel(tc, x_words, x_scales, w1, d_words
             nc.sync.dma_start(tile[:].bitcast(I32), src[0].rearrange("p c r -> p (c r)").bitcast(I32))
             return tile
 
-        def load_weight(name, src):
-            tile = keep.tile([P, PACK, H], F32, name=name, align_bytes=64)
+        def load_weight(name, src, tag=None):
+            tile = keep.tile([P, PACK, H], F32, name=name, tag=tag or name, align_bytes=64)
             nc.sync.dma_start(tile[:], src.rearrange("(p j) c -> p j c", j=PACK))
             return tile
 
@@ -60,13 +60,12 @@ def tile_picked_twkeypathbhinge_none_p_kernel(tc, x_words, x_scales, w1, d_words
         x_table = load_words("x_table", x_words)
         two_t = load_list("two_t", two)
         d_table = load_words("d_table", d_words)
-        n3_t = load_list("n3_t", n3)
         n1_t = load_list("n1_t", n1)
-        n4_t = load_list("n4_t", n4)
+        n3_t = load_list("n3_t", n3)
         n2_t = load_list("n2_t", n2)
+        n4_t = load_list("n4_t", n4)
         gain = keep.tile([P, PACK], F32, name="gain")
         nc.sync.dma_start(gain[:], gn.rearrange("(p t) o -> p (t o)", t=PACK))
-        w2_raw = load_weight("w2_raw", w2)
         n5_t = load_list("n5_t", n5)
         n6_t = load_list("n6_t", n6)
 
@@ -109,77 +108,168 @@ def tile_picked_twkeypathbhinge_none_p_kernel(tc, x_words, x_scales, w1, d_words
         def entries(offsets, lo, width):
             return offsets[:, lo // LIST_COL : (lo + width) // LIST_COL]
 
+        def window(name, wide):
+            tile = keep.tile([P, 2 * S if wide else S], F32, name=name, align_bytes=64)
+            if wide:
+                nc.gpsimd.memset(tile[:, S:], 0.0)
+            return tile
+
+        last = PACK - 1
+        y_sb = [window("y%d" % t, True) for t in range(last)]
+        d_sb = [window("d%d" % t, t < last) for t in range(PACK)]
+        h_sb = [y_sb[0], y_sb[1], y_sb[2], window("h3", False)]
+        y_banks = []
+
         dk_bytes_picked = pick("dk_bytes_picked", d_bytes, k1_t, U8)
         dk_bytes = deal("dk_bytes", dk_bytes_picked, U8)
         for e in range(1, 4):
             nc.sync.dma_start(dk_bytes[e:P:32, :].bitcast(I32), dk_bytes[8 * e : P : 32, :].bitcast(I32))
+        w2_raw = load_weight("w2_raw", w2, "dk_bytes_picked")
         xo_bytes = pick("xo_bytes", x_bytes, offs_t, U8)
-        w1_bf = round_weight(nc.scalar.copy, "w1_bf", w1_raw, "w1_bf")
+        w1_bf = []
         xt_bytes = pick("xt_bytes", x_bytes, two_t, U8)
+        for a, copy in enumerate((nc.scalar.copy, nc.vector.tensor_copy)):
+            tile = keep.tile([P, 2 * H], BF16, name="w1_bf%d" % a, align_bytes=64)
+            copy(
+                tile[:].rearrange("p (t m j) -> p m j t", t=2, j=PACK),
+                w1_raw[:].rearrange("p j (m t) -> p m j t", t=PACK)[:, :, :, 2 * a : 2 * a + 2],
+            )
+            w1_bf.append(tile)
+        w1_q = [quantize("w1a", w1_bf[0], H // 2), quantize("w1b", w1_bf[1], H // 2)]
         xo_words = pick("xo_words", x_table, offs_t, U32)
-        w1_q = quantize("w1", w1_bf, H)
 
-        y_sb, d_sb = [], []
         for t in range(PACK):
             bank = psum.tile([P, S], F32, name="ybank%d" % t, tag="bank%d" % t)
-            product(bank[:], w1_q, t, (xo_words, xo_bytes))
-            tile = keep.tile([P, S], F32, name="y%d" % t, align_bytes=64)
-            nc.scalar.copy(tile[:], bank[:])
-            y_sb.append(tile)
+            product(bank[:], w1_q[t // 2], t % 2, (xo_words, xo_bytes))
+            y_banks.append(bank)
+            if t < last:
+                nc.scalar.copy(y_sb[t][:, :S], bank[:])
 
-        xt_words = pick("xt_words", x_table, two_t, U32, "w1_bf")
+        xt_words = pick("xt_words", x_table, two_t, U32, "w1_bf1")
         dk_words_picked = pick("dk_words_picked", d_table, k1_t, U32, "x_table")
         dk_words = deal("dk_words", dk_words_picked, U32)
+        y_sb.append(keep.tile([P, S], F32, name="y3", tag="x_table", align_bytes=64))
+        nc.vector.tensor_copy(y_sb[last][:], y_banks[last][:])
         w2_bf = round_weight(nc.vector.tensor_copy, "w2_bf", w2_raw, "d_table")
-        w2_q = quantize("w2", w2_bf, N)
         for t in range(PACK):
             bank = psum.tile([P, S], F32, name="dbank%d" % t, tag="bank%d" % (PACK + t))
             product(bank[:], (dk_words, dk_bytes), t, (xt_words, xt_bytes))
-            tile = keep.tile([P, S], F32, name="d%d" % t, align_bytes=64)
-            if t < 1:
-                nc.vector.tensor_scalar(tile[:], bank[:], 0.0625, None, ALU.mult)
+            if t < 0:
+                nc.vector.tensor_scalar(d_sb[t][:, :S], bank[:], 0.0625, None, ALU.mult)
             else:
-                nc.scalar.activation(tile[:], bank[:], ACT.Copy, scale=0.0625)
-            d_sb.append(tile)
+                nc.scalar.activation(d_sb[t][:, :S], bank[:], ACT.Copy, scale=0.0625)
 
-        h_banks = [psum.tile([P, S], F32, name="hbank%d" % t, tag="bank%d" % t) for t in range(PACK)]
-        h_sb = [keep.tile([P, S], F32, name="h%d" % t, align_bytes=64) for t in range(PACK)]
-        lo = 0
-        for c, width in enumerate(MID):
-            cols = slice(lo, lo + width)
-            larger = keep.tile([P, PACK, width], F32, name="larger%d" % c, align_bytes=64)
-            for t in range(PACK):
-                sums = []
-                for u, (ny, nd) in enumerate(((n1_t, n3_t), (n2_t, n4_t))):
-                    yg = keep.tile([P, width], F32, name="yg", tag="yg", bufs=YG_BUFS, align_bytes=64)
-                    nc.scalar.activation(yg[:], y_sb[t][:].indirect(entries(ny, lo, width)), ACT.Copy)
-                    sm = keep.tile([P, width], F32, name="sum", tag="sum", bufs=4, align_bytes=64)
-                    if c == 0 or (u == 0 and t % 2 == 0):
-                        nc.vector.tensor_tensor(sm[:], d_sb[t][:].indirect(entries(nd, lo, width)), yg[:], ALU.add)
-                    else:
-                        dg = keep.tile([P, width], F32, name="dg", tag="dg", bufs=DG_BUFS, align_bytes=64)
-                        nc.scalar.activation(dg[:], d_sb[t][:].indirect(entries(nd, lo, width)), ACT.Copy)
-                        nc.vector.tensor_tensor(sm[:], dg[:], yg[:], ALU.add)
-                    sums.append(sm)
-                nc.vector.tensor_tensor(larger[:, t, :], sums[0][:], sums[1][:], ALU.max)
-            z_bf = keep.tile([P, PACK * width], BF16, name="z_bf%d" % c, align_bytes=64)
-            nc.vector.tensor_tensor(
+        def fetch(dst, win, offsets):
+            nc.scalar.activation(dst, win[:].indirect(offsets), ACT.Copy)
+
+        def staged(shape, tag):
+            return keep.tile(shape, F32, name=tag, tag=tag, align_bytes=64)
+
+        larger = keep.tile([P, PACK, S], F32, name="larger", align_bytes=64)
+        pairs = ((n1_t, n3_t), (n2_t, n4_t))
+        def fetch_y(t, lo, width, tag):
+            yg = staged([P, 2, width], tag)
+            for u in range(2):
+                fetch(yg[:, u, :], y_sb[t], entries(pairs[u][0], lo, width))
+            return yg
+
+        def fetch_d(t, lo, width, first, tag):
+            dg = staged([P, 2, width], tag)
+            for u in range(first, 2):
+                fetch(dg[:, u, :], d_sb[t], entries(pairs[u][1], lo, width))
+            return dg
+
+        def sum_tile(t, lo, width):
+            return keep.tile([P, 2, width], F32, name="sums%d_%d" % (t, lo), align_bytes=64)
+
+        def add_fetched(sums, u, t, lo, width, yg):
+            nc.vector.tensor_tensor(sums[:, u, :], d_sb[t][:].indirect(entries(pairs[u][1], lo, width)), yg, ALU.add)
+
+        def add_plain(sums, yg, dg, first):
+            nc.vector.tensor_tensor(sums[:, first:, :], yg[:, first:, :], dg[:, first:, :], ALU.add)
+
+        def take_larger(sums, t, lo, width):
+            nc.vector.tensor_tensor(larger[:, t, lo : lo + width], sums[:, 0, :], sums[:, 1, :], ALU.max)
+
+        z_rows = keep.tile([P, PACK, S], BF16, name="z_rows", align_bytes=64)
+
+        def gain_round(t, lo, width):
+            nc.vector.tensor_scalar(z_rows[:, t, lo : lo + width], larger[:, t, lo : lo + width], gain[:, t : t + 1], None, ALU.mult)
+
+        def scale_round(lo, width):
+            z_bf = keep.tile([P, PACK * width], BF16, name="z_bf%d" % lo, align_bytes=64)
+            nc.vector.tensor_copy(
                 z_bf[:].rearrange("p (b i t) -> p b t i", i=4, t=PACK),
-                larger[:].rearrange("p t (b i) -> p b t i", i=4),
-                gain[:].unsqueeze(1).unsqueeze(3).to_broadcast([P, width // 4, PACK, 4]),
-                ALU.mult,
+                z_rows[:, :, lo : lo + width].rearrange("p t (b i) -> p b t i", i=4),
             )
-            z_q = quantize("z%d" % c, z_bf, width)
+            return z_bf
+
+        def second_layer(z_bf, lo, width, first_bank):
+            z_q = quantize("z%d" % lo, z_bf, width)
+            banks = [psum.tile([P, width], F32, name="hbank", tag="bank%d" % (first_bank + t)) for t in range(PACK)]
             for t in range(PACK):
-                product(h_banks[t][:, cols], w2_q, t, z_q)
-                nc.scalar.activation(h_sb[t][:, cols], h_banks[t][:, cols], ACT.Copy, scale=-1.0)
-            lo = lo + width
+                product(banks[t][:], w2_q, t, z_q)
+            return banks
+
+        def leave(banks, lo, width, on_vector):
+            for t in range(PACK):
+                if t < on_vector:
+                    nc.vector.tensor_scalar(h_sb[t][:, lo : lo + width], banks[t][:], -1.0, None, ALU.mult)
+                else:
+                    nc.scalar.activation(h_sb[t][:, lo : lo + width], banks[t][:], ACT.Copy, scale=-1.0)
+
+        Q = HALF // 2
+
+        def whole_pair(sums, t, u, tag):
+            yg = staged([P, S], tag)
+            fetch(yg[:], y_sb[t], pairs[u][0][:])
+            add_fetched(sums, u, t, 0, S, yg[:])
+
+        s0, s1, s2 = sum_tile(0, 0, S), sum_tile(1, 0, S), sum_tile(2, 0, S)
+        whole_pair(s0, 0, 0, "first0")
+        w2_q = quantize("w2", w2_bf, N)
+        whole_pair(s0, 0, 1, "first1")
+        whole_pair(s1, 1, 0, "dk_words")
+        take_larger(s0, 0, 0, S)
+        whole_pair(s1, 1, 1, "w1_bf1")
+        gain_round(0, 0, S)
+        whole_pair(s2, 2, 0, "first0")
+        take_larger(s1, 1, 0, S)
+        y21, d21 = staged([P, S], "first1"), staged([P, S], "d_table")
+        fetch(y21[:], y_sb[2], pairs[1][0][:])
+        fetch(d21[:], d_sb[2], pairs[1][1][:])
+        nc.vector.tensor_tensor(s2[:, 1, :], y21[:], d21[:], ALU.add)
+        gain_round(1, 0, S)
+        y3a, d3a = fetch_y(3, 0, HALF, "dk_words"), fetch_d(3, 0, HALF, 0, "sums0_0")
+        y3b, d3b = fetch_y(3, HALF, Q, "w1_bf1"), fetch_d(3, HALF, Q, 0, "sums1_0")
+        y3c, d3c = fetch_y(3, HALF + Q, Q, "first0"), fetch_d(3, HALF + Q, Q, 0, "first1")
+        s3a, s3b, s3c = sum_tile(3, 0, HALF), sum_tile(3, HALF, Q), sum_tile(3, HALF + Q, Q)
+        add_plain(s3a, y3a, d3a, 0)
+        take_larger(s2, 2, 0, S)
+        take_larger(s3a, 3, 0, HALF)
+        gain_round(2, 0, S)
+        gain_round(3, 0, HALF)
+        add_plain(s3b, y3b, d3b, 0)
+        za = scale_round(0, HALF)
+        take_larger(s3b, 3, HALF, Q)
+        ha = second_layer(za, 0, HALF, 0)
+        gain_round(3, HALF, Q)
+        add_plain(s3c, y3c, d3c, 0)
+        zb = scale_round(HALF, Q)
+        take_larger(s3c, 3, HALF + Q, Q)
+        hb = second_layer(zb, HALF, Q, PACK)
+        gain_round(3, HALF + Q, Q)
+        leave(ha, 0, HALF, 0)
+        zc = scale_round(HALF + Q, Q)
+        hc = second_layer(zc, HALF + Q, Q, 0)
+        leave(hb, HALF, Q, 0)
+        leave(hc, HALF + Q, Q, 1)
 
         out_rows = out.rearrange("(p t) j -> p t j", t=PACK)
         pieces = []
         for t in range(PACK):
             lo = 0
-            for width in (LAST if t == PACK - 1 else (WIDE, WIDE)):
+            for width in ((S,), (S,), (HALF, HALF), LAST)[t]:
                 pieces.append((t, lo, width))
                 lo = lo + width
 
@@ -191,11 +281,14 @@ def tile_picked_twkeypathbhinge_none_p_kernel(tc, x_words, x_scales, w1, d_words
         pending = None
         for k, (t, lo, width) in enumerate(pieces):
             got = keep.tile([P, 2, width], F32, name="got%d" % k, align_bytes=64)
-            if k < 2 or k == len(pieces) - 1:
+            if k == 0:
                 nc.vector.tensor_copy(got[:, 0, :], h_sb[t][:].indirect(entries(n5_t, lo, width)))
+            elif k == 1:
+                nc.vector.tensor_copy(got[:, 0, :HALF], h_sb[t][:].indirect(entries(n5_t, 0, HALF)))
+                fetch(got[:, 0, HALF:], h_sb[t], entries(n5_t, HALF, HALF))
             else:
-                nc.scalar.activation(got[:, 0, :], h_sb[t][:].indirect(entries(n5_t, lo, width)), ACT.Copy)
-            nc.scalar.activation(got[:, 1, :], h_sb[t][:].indirect(entries(n6_t, lo, width)), ACT.Copy)
+                fetch(got[:, 0, :], h_sb[t], entries(n5_t, lo, width))
+            fetch(got[:, 1, :], h_sb[t], entries(n6_t, lo, width))
             diff = keep.tile([P, 2, width], F32, name="diff%d" % k, align_bytes=64)
             nc.vector.tensor_tensor(diff[:], got[:], h_sb[t][:, lo : lo + width].unsqueeze(1).to_broadcast([P, 2, width]), ALU.subtract)
             if pending is not None:

from contextlib import ExitStack

import concourse.mybir as mybir

K, T, S, H, N = 512, 2048, 512, 512, 512
FLOPS = 3 * 2 * 512 * 512 * 512

F32 = mybir.dt.float32
BF16 = mybir.dt.bfloat16
I32 = mybir.dt.int32
U32 = mybir.dt.uint32
U16 = mybir.dt.uint16
U8 = mybir.dt.uint8
FP8X4 = mybir.dt.float8_e4m3fn_x4
ALU = mybir.AluOpType
ACT = mybir.ActivationFunctionType

P = 128
PACK = 4
MID = ((256,), (128, 128))
WHOLE = 2
HALF = 256
GOT_BUFS = 4
LAST = (256, 128, 128)
LIST_COL = 16


def tile_picked_twkeypathbhinge_none_p_kernel(tc, x_words, x_scales, w1, d_words, d_scales, gn, w2, offs, k1, two, n1, n2, n3, n4, n5, n6, out):
    nc = tc.nc
    with ExitStack() as ctx:
        keep = ctx.enter_context(tc.tile_pool(name="keep", bufs=1))
        psum = ctx.enter_context(tc.psum_pool(name="psum", bufs=1))

        def load_list(name, src):
            tile = keep.tile([P, S // LIST_COL], U16, name=name)
            nc.sync.dma_start(tile[:], src)
            return tile

        def load_words(name, src):
            tile = keep.tile([P, T], U32, name=name, align_bytes=64)
            nc.sync.dma_start(tile[:].bitcast(I32), src[0].rearrange("p c r -> p (c r)").bitcast(I32))
            return tile

        def load_weight(name, src, tag=None):
            tile = keep.tile([P, PACK, H], F32, name=name, tag=tag or name, align_bytes=64)
            nc.sync.dma_start(tile[:], src.rearrange("(p j) c -> p j c", j=PACK))
            return tile

        k1_t = load_list("k1_t", k1)
        d_bytes = keep.tile([P, T], U8, name="d_bytes", align_bytes=64)
        nc.sync.dma_start(d_bytes[:].bitcast(I32), d_scales[0].bitcast(I32).unsqueeze(1).to_broadcast([16, 8, T // 4]))
        offs_t = load_list("offs_t", offs)
        x_bytes = keep.tile([P, T], U8, name="x_bytes", align_bytes=64)
        for q in range(4):
            nc.sync.dma_start(
                x_bytes[32 * q : 32 * q + 32, :].bitcast(I32),
                x_scales[0, 4 * q : 4 * q + 4, :].bitcast(I32).unsqueeze(0).to_broadcast([8, 4, T // 4]),
            )
        w1_raw = load_weight("w1_raw", w1)
        x_table = load_words("x_table", x_words)
        two_t = load_list("two_t", two)
        d_table = load_words("d_table", d_words)
        n1_t = load_list("n1_t", n1)
        n3_t = load_list("n3_t", n3)
        n2_t = load_list("n2_t", n2)
        n4_t = load_list("n4_t", n4)
        gain = keep.tile([P, PACK], F32, name="gain")
        nc.sync.dma_start(gain[:], gn.rearrange("(p t) o -> p (t o)", t=PACK))
        n5_t = load_list("n5_t", n5)
        n6_t = load_list("n6_t", n6)

        def pick(name, table, offsets, dtype, tag=None):
            tile = keep.tile([P, S], dtype, name=name, tag=tag or name, align_bytes=64)
            nc.vector.tensor_copy(tile[:], table[:].indirect(offsets[:]))
            return tile

        def deal(name, picked, dtype):
            tile = keep.tile([P, S], dtype, name=name, align_bytes=64)
            nc.vector.tensor_copy(tile[:].rearrange("p (t m) -> p m t", t=PACK), picked[:].rearrange("p (m t) -> p m t", t=PACK))
            return tile

        def round_weight(copy, name, raw, tag):
            tile = keep.tile([P, PACK * H], BF16, name=name, tag=tag, align_bytes=64)
            copy(
                tile[:].rearrange("p (t m j) -> p m j t", t=PACK, j=PACK),
                raw[:].rearrange("p j (m t) -> p m j t", t=PACK),
            )
            return tile

        def quantize(name, rounded, width):
            codes = keep.tile([P, width], U32, name=name + "_codes", align_bytes=64)
            scales = keep.tile([P, width], U8, name=name + "_scales", align_bytes=64)
            nc.vector.quantize_mx(out=codes[:].bitcast(FP8X4), scales=scales[:], in_=rounded[:])
            return codes, scales

        def product(bank_cols, lhs, t, rhs):
            cols = slice(P * t, P * (t + 1))
            nc.tensor.matmul_mx(
                out=bank_cols,
                lhsT=lhs[0][:, cols].bitcast(FP8X4),
                lhsT_scale=lhs[1][:, cols],
                rhs=rhs[0][:].bitcast(FP8X4),
                rhs_scale=rhs[1][:],
                start=True,
                stop=True,
            )

        def entries(offsets, lo, width):
            return offsets[:, lo // LIST_COL : (lo + width) // LIST_COL]

        def window(name, wide):
            tile = keep.tile([P, 2 * S if wide else S], F32, name=name, align_bytes=64)
            if wide:
                nc.gpsimd.memset(tile[:, S:], 0.0)
            return tile

        last = PACK - 1
        y_sb = [window("y%d" % t, True) for t in range(last)]
        d_sb = [window("d%d" % t, t < last) for t in range(PACK)]
        h_sb = [y_sb[0], y_sb[1], y_sb[2], window("h3", False)]
        y_banks = []

        dk_bytes_picked = pick("dk_bytes_picked", d_bytes, k1_t, U8)
        dk_bytes = deal("dk_bytes", dk_bytes_picked, U8)
        for e in range(1, 4):
            nc.sync.dma_start(dk_bytes[e:P:32, :].bitcast(I32), dk_bytes[8 * e : P : 32, :].bitcast(I32))
        w2_raw = load_weight("w2_raw", w2, "dk_bytes_picked")
        xo_bytes = pick("xo_bytes", x_bytes, offs_t, U8)
        w1_bf = []
        xt_bytes = pick("xt_bytes", x_bytes, two_t, U8)
        for a, copy in enumerate((nc.scalar.copy, nc.vector.tensor_copy)):
            tile = keep.tile([P, 2 * H], BF16, name="w1_bf%d" % a, align_bytes=64)
            copy(
                tile[:].rearrange("p (t m j) -> p m j t", t=2, j=PACK),
                w1_raw[:].rearrange("p j (m t) -> p m j t", t=PACK)[:, :, :, 2 * a : 2 * a + 2],
            )
            w1_bf.append(tile)
        w1_q = [quantize("w1a", w1_bf[0], H // 2), quantize("w1b", w1_bf[1], H // 2)]
        xo_words = pick("xo_words", x_table, offs_t, U32)

        for t in range(PACK):
            bank = psum.tile([P, S], F32, name="ybank%d" % t, tag="bank%d" % t)
            product(bank[:], w1_q[t // 2], t % 2, (xo_words, xo_bytes))
            y_banks.append(bank)
            if t < last:
                nc.scalar.copy(y_sb[t][:, :S], bank[:])

        xt_words = pick("xt_words", x_table, two_t, U32, "w1_bf1")
        dk_words_picked = pick("dk_words_picked", d_table, k1_t, U32, "x_table")
        dk_words = deal("dk_words", dk_words_picked, U32)
        y_sb.append(keep.tile([P, S], F32, name="y3", tag="x_table", align_bytes=64))
        nc.vector.tensor_copy(y_sb[last][:], y_banks[last][:])
        w2_bf = round_weight(nc.vector.tensor_copy, "w2_bf", w2_raw, "d_table")
        for t in range(PACK):
            bank = psum.tile([P, S], F32, name="dbank%d" % t, tag="bank%d" % (PACK + t))
            product(bank[:], (dk_words, dk_bytes), t, (xt_words, xt_bytes))
            if t < 0:
                nc.vector.tensor_scalar(d_sb[t][:, :S], bank[:], 0.0625, None, ALU.mult)
            else:
                nc.scalar.activation(d_sb[t][:, :S], bank[:], ACT.Copy, scale=0.0625)

        def fetch(dst, win, offsets):
            nc.scalar.activation(dst, win[:].indirect(offsets), ACT.Copy)

        def staged(shape, tag):
            return keep.tile(shape, F32, name=tag, tag=tag, align_bytes=64)

        larger = keep.tile([P, PACK, S], F32, name="larger", align_bytes=64)
        pairs = ((n1_t, n3_t), (n2_t, n4_t))
        def fetch_y(t, lo, width, tag):
            yg = staged([P, 2, width], tag)
            for u in range(2):
                fetch(yg[:, u, :], y_sb[t], entries(pairs[u][0], lo, width))
            return yg

        def fetch_d(t, lo, width, first, tag):
            dg = staged([P, 2, width], tag)
            for u in range(first, 2):
                fetch(dg[:, u, :], d_sb[t], entries(pairs[u][1], lo, width))
            return dg

        def sum_tile(t, lo, width):
            return keep.tile([P, 2, width], F32, name="sums%d_%d" % (t, lo), align_bytes=64)

        def add_fetched(sums, u, t, lo, width, yg):
            nc.vector.tensor_tensor(sums[:, u, :], d_sb[t][:].indirect(entries(pairs[u][1], lo, width)), yg, ALU.add)

        def add_plain(sums, yg, dg, first):
            nc.vector.tensor_tensor(sums[:, first:, :], yg[:, first:, :], dg[:, first:, :], ALU.add)

        def take_larger(sums, t, lo, width):
            nc.vector.tensor_tensor(larger[:, t, lo : lo + width], sums[:, 0, :], sums[:, 1, :], ALU.max)

        z_rows = keep.tile([P, PACK, S], BF16, name="z_rows", align_bytes=64)

        def gain_round(t, lo, width):
            nc.vector.tensor_scalar(z_rows[:, t, lo : lo + width], larger[:, t, lo : lo + width], gain[:, t : t + 1], None, ALU.mult)

        def scale_round(lo, width):
            z_bf = keep.tile([P, PACK * width], BF16, name="z_bf%d" % lo, align_bytes=64)
            nc.vector.tensor_copy(
                z_bf[:].rearrange("p (b i t) -> p b t i", i=4, t=PACK),
                z_rows[:, :, lo : lo + width].rearrange("p t (b i) -> p b t i", i=4),
            )
            return z_bf

        def second_layer(z_bf, lo, width, first_bank):
            z_q = quantize("z%d" % lo, z_bf, width)
            banks = [psum.tile([P, width], F32, name="hbank", tag="bank%d" % (first_bank + t)) for t in range(PACK)]
            for t in range(PACK):
                product(banks[t][:], w2_q, t, z_q)
            return banks

        def leave(banks, lo, width, on_vector):
            for t in range(PACK):
                if t < on_vector:
                    nc.vector.tensor_scalar(h_sb[t][:, lo : lo + width], banks[t][:], -1.0, None, ALU.mult)
                else:
                    nc.scalar.activation(h_sb[t][:, lo : lo + width], banks[t][:], ACT.Copy, scale=-1.0)

        Q = HALF // 2

        def whole_pair(sums, t, u, tag):
            yg = staged([P, S], tag)
            fetch(yg[:], y_sb[t], pairs[u][0][:])
            add_fetched(sums, u, t, 0, S, yg[:])

        s0, s1, s2 = sum_tile(0, 0, S), sum_tile(1, 0, S), sum_tile(2, 0, S)
        whole_pair(s0, 0, 0, "first0")
        w2_q = quantize("w2", w2_bf, N)
        whole_pair(s0, 0, 1, "first1")
        whole_pair(s1, 1, 0, "dk_words")
        take_larger(s0, 0, 0, S)
        whole_pair(s1, 1, 1, "w1_bf1")
        gain_round(0, 0, S)
        whole_pair(s2, 2, 0, "first0")
        take_larger(s1, 1, 0, S)
        y21, d21 = staged([P, S], "first1"), staged([P, S], "d_table")
        fetch(y21[:], y_sb[2], pairs[1][0][:])
        fetch(d21[:], d_sb[2], pairs[1][1][:])
        nc.vector.tensor_tensor(s2[:, 1, :], y21[:], d21[:], ALU.add)
        gain_round(1, 0, S)
        y3a, d3a = fetch_y(3, 0, HALF, "dk_words"), fetch_d(3, 0, HALF, 0, "sums0_0")
        y3b, d3b = fetch_y(3, HALF, Q, "w1_bf1"), fetch_d(3, HALF, Q, 0, "sums1_0")
        y3c, d3c = fetch_y(3, HALF + Q, Q, "first0"), fetch_d(3, HALF + Q, Q, 0, "first1")
        s3a, s3b, s3c = sum_tile(3, 0, HALF), sum_tile(3, HALF, Q), sum_tile(3, HALF + Q, Q)
        add_plain(s3a, y3a, d3a, 0)
        take_larger(s2, 2, 0, S)
        take_larger(s3a, 3, 0, HALF)
        gain_round(2, 0, S)
        gain_round(3, 0, HALF)
        add_plain(s3b, y3b, d3b, 0)
        za = scale_round(0, HALF)
        take_larger(s3b, 3, HALF, Q)
        ha = second_layer(za, 0, HALF, 0)
        gain_round(3, HALF, Q)
        add_plain(s3c, y3c, d3c, 0)
        zb = scale_round(HALF, Q)
        take_larger(s3c, 3, HALF + Q, Q)
        hb = second_layer(zb, HALF, Q, PACK)
        gain_round(3, HALF + Q, Q)
        leave(ha, 0, HALF, 0)
        zc = scale_round(HALF + Q, Q)
        hc = second_layer(zc, HALF + Q, Q, 0)
        leave(hb, HALF, Q, 0)
        leave(hc, HALF + Q, Q, 1)

        out_rows = out.rearrange("(p t) j -> p t j", t=PACK)
        pieces = []
        for t in range(PACK):
            lo = 0
            for width in ((S,), (S,), (HALF, HALF), LAST)[t]:
                pieces.append((t, lo, width))
                lo = lo + width

        def finish(k, t, lo, width, diff, half):
            res = keep.tile([P, width], F32, name="res%d" % k, align_bytes=64)
            nc.vector.scalar_tensor_tensor(res[:], diff[:, 0, :], 0.0, half[:], ALU.max, ALU.add)
            nc.sync.dma_start(out_rows[:, t, lo : lo + width], res[:])

        pending = None
        for k, (t, lo, width) in enumerate(pieces):
            got = keep.tile([P, 2, width], F32, name="got%d" % k, align_bytes=64)
            if k == 0:
                nc.vector.tensor_copy(got[:, 0, :], h_sb[t][:].indirect(entries(n5_t, lo, width)))
            elif k == 1:
                nc.vector.tensor_copy(got[:, 0, :HALF], h_sb[t][:].indirect(entries(n5_t, 0, HALF)))
                fetch(got[:, 0, HALF:], h_sb[t], entries(n5_t, HALF, HALF))
            else:
                fetch(got[:, 0, :], h_sb[t], entries(n5_t, lo, width))
            fetch(got[:, 1, :], h_sb[t], entries(n6_t, lo, width))
            diff = keep.tile([P, 2, width], F32, name="diff%d" % k, align_bytes=64)
            nc.vector.tensor_tensor(diff[:], got[:], h_sb[t][:, lo : lo + width].unsqueeze(1).to_broadcast([P, 2, width]), ALU.subtract)
            if pending is not None:
                finish(*pending)
            half = keep.tile([P, width], F32, name="half%d" % k, align_bytes=64)
            nc.vector.tensor_scalar(half[:], diff[:, 1, :], 0.0, -0.5, ALU.min, ALU.mult)
            pending = (k, t, lo, width, diff, half)
        finish(*pending)
